import numpy as np
import ml_dtypes


def mxq(x, axis, fmt="e4m3"):
    dtype, down = {"e4m3": (ml_dtypes.float8_e4m3fn, 7), "e5m2": (ml_dtypes.float8_e5m2, 14)}[fmt]
    v = np.moveaxis(np.asarray(x, np.float32).astype(ml_dtypes.bfloat16).astype(np.float64), axis, -1)
    blocks = v.reshape(v.shape[:-1] + (-1, 32))
    amax = np.abs(blocks).max(-1, keepdims=True)
    byte = np.maximum(np.where(amax > 0, np.frexp(amax)[1] - 1 + 127, 0) - down, 1)
    scale = np.exp2(byte - 127.0)
    codes = (blocks / scale).astype(np.float32).astype(dtype).astype(np.float64)
    return np.moveaxis((codes * scale).reshape(v.shape), -1, axis)


WIDE = False


def mx_kscale(k):
    if not WIDE:
        return np.ones(k)
    levels = np.array([10, -10, 5, -5, 0])
    if k % 512:
        return np.exp2(np.random.permutation(np.resize(levels, k // 32))).repeat(32)
    a = np.empty((k // 512, 16))
    for p in range(k // 512):
        a[p, :8] = np.random.permutation(np.resize(levels, 8))
        for g in range(8):
            far = levels[np.abs(levels - a[p, g]) >= 10]
            a[p, g + 8] = far[np.random.randint(len(far))]
    return np.exp2(a.ravel()).repeat(32)


def f64(x):
    return np.asarray(x).astype(np.float64)


def striped(idx):
    return np.tile(idx.reshape(-1, 16).T, (8, 1)).astype(np.uint16)


def unstriped(offs):
    return offs[:16].T.reshape(-1).astype(np.int64)


def pack_weight(w):
    k, n = w.shape
    w = f64(np.asarray(w, np.float32).astype(ml_dtypes.bfloat16)).reshape(k // 32, 32, n)
    amax = np.abs(w).max(1)
    byte = np.clip(np.where(amax > 0, np.frexp(amax)[1] - 1 + 127 - 7, 1), 1, 254)
    scaled = (w * np.exp2(127.0 - byte)[:, None, :]).reshape(k, n).astype(np.float32)
    words = np.ascontiguousarray(scaled.reshape(k // 512, 128, 4, n).transpose(0, 1, 3, 2)).astype(ml_dtypes.float8_e4m3fn).view(np.uint8)
    return words, np.ascontiguousarray(byte.astype(np.uint8).reshape(k // 512, 16, n))


def unpack_weight(words, scales):
    g, p, n, _ = words.shape
    vals = np.ascontiguousarray(words).view(ml_dtypes.float8_e4m3fn).astype(np.float64) * np.repeat(np.exp2(scales.astype(np.float64) - 127.0), 8, axis=1)[..., None]
    return vals.transpose(0, 1, 3, 2).reshape(g * 512, n)


K, T, S, D, N = 512, 2048, 1024, 4, 256
P = 2 ** 7


def setup_inputs():
    n = np.random.standard_normal
    s = mx_kscale(K)[:, None]
    packed_xT = pack_weight(n((K, T)) * s)
    return {
        "x_words": packed_xT[0],
        "x_scales": packed_xT[1],
        "w1": (n((K, N)) / np.sqrt(K) / s).astype(np.float32),
        "cnt": (np.tile(np.floor(np.random.uniform(0.0, 20.0, S)), (P, 1))).astype(np.float32),
        "qv": (np.random.uniform(-1.0, 1.0, (N, S))).astype(np.float32),
        "cpu": (np.random.uniform(0.8, 2.5, (N, 1))).astype(np.float32),
        "offs": striped(np.random.permutation(T)[:S]),
    }


def reference(x_words, x_scales, w1, cnt, qv, cpu, offs):
    xq = unpack_weight(x_words, x_scales)[:, unstriped(offs)]
    y = mxq(f64(w1), 0, "e4m3").T @ xq
    top = y.reshape(len(y), -1, D).max(axis=2)
    ex = np.exp(y - np.repeat(top, D, axis=1))
    total = ex.reshape(len(ex), -1, D).sum(axis=2)
    pri = ex / np.repeat(total, D, axis=1)
    tot = np.sqrt(f64(cnt)[:1].reshape(len(f64(cnt)[:1]), -1, D).sum(axis=2) + 1.0)
    return f64(qv) + f64(cpu) * ((pri * np.repeat(tot, D, axis=1)) / (f64(cnt)[:1] + 1.0))

@@ -1,0 +1,192 @@
+from contextlib import ExitStack
+
+import concourse.mybir as mybir
+from concourse.masks import make_identity
+
+K, T, S, D, N = 512, 2048, 1024, 4, 256
+FLOPS = 2 * K * N * S
+BYTES = K * T + (K // 32) * T + 4 * K * N + 4 * S + 4 * N * S + 4 * N + 128 * (S // 16) * 2 + 4 * N * S
+
+F32 = mybir.dt.float32
+BF16 = mybir.dt.bfloat16
+I32 = mybir.dt.int32
+U32 = mybir.dt.uint32
+U16 = mybir.dt.uint16
+U8 = mybir.dt.uint8
+FP8X4 = mybir.dt.float8_e4m3fn_x4
+ALU = mybir.AluOpType
+ACT = mybir.ActivationFunctionType
+AX = mybir.AxisListType
+
+P = 128
+PACK = 4
+HALF = 512
+HALVES = S // HALF
+BLOCKS = N // P
+
+
+def tile_picked_ypuct_puct_p_kernel(tc, x_words, x_scales, w1, cnt, qv, cpu, offs, out):
+    nc = tc.nc
+    with ExitStack() as ctx:
+        keep = ctx.enter_context(tc.tile_pool(name="keep", bufs=1))
+        psum = ctx.enter_context(tc.psum_pool(name="psum", bufs=1))
+        banks = [psum.tile([P, HALF], F32, name="bank%d" % i) for i in range(8)]
+
+        offsets = keep.tile([P, S // 16], U16, name="offsets")
+        nc.sync.dma_start(offsets[:], offs)
+
+        visits = keep.tile([P, HALVES, D], F32, name="visits")
+        nc.sync.dma_start(out=visits[:], in_=cnt[0, :].rearrange("(h p d) -> p h d", h=HALVES, d=D))
+
+        table_scales = keep.tile([P, T], U8, name="table_scales", align_bytes=64)
+        nc.vector.memset(table_scales[:].bitcast(I32), 0)
+        for q in range(4):
+            nc.sync.dma_start(out=table_scales[32 * q : 32 * q + 4, :].bitcast(I32), in_=x_scales[0, 4 * q : 4 * q + 4, :].bitcast(I32))
+
+        w_raw = keep.tile([P, PACK, N], F32, name="w_raw")
+        nc.sync.dma_start(out=w_raw[:], in_=w1.rearrange("(p j) m -> p j m", j=PACK))
+        table_words = keep.tile([P, T], U32, name="table_words", align_bytes=64)
+        nc.sync.dma_start(out=table_words[:].bitcast(I32), in_=x_words[0].rearrange("p c r -> p (c r)").bitcast(I32))
+
+        explore = keep.tile([P, BLOCKS], F32, name="explore")
+        with nc.allow_non_contiguous_dma(reason="one value a partition"):
+            nc.sync.dma_start(out=explore[:], in_=cpu.rearrange("(b p) o -> p (b o)", b=BLOCKS))
+        values = [keep.tile([P, S], F32, name="values%d" % b) for b in range(BLOCKS)]
+        for b in range(BLOCKS):
+            nc.sync.dma_start(out=values[b][:], in_=qv[b * P : (b + 1) * P, :])
+
+        ident = keep.tile([P, P], F32, name="ident")
+        make_identity(nc, ident[:])
+
+        visits1 = keep.tile([P, HALVES, D], F32, name="visits1")
+        inv_visits = keep.tile([P, HALVES, D], F32, name="inv_visits")
+        node_visits = keep.tile([P, HALVES], F32, name="node_visits")
+        node_visits1 = keep.tile([P, HALVES], F32, name="node_visits1")
+        one_half = keep.tile([P, HALVES], F32, name="one_half")
+        root = keep.tile([P, HALVES], F32, name="root")
+        nc.vector.tensor_reduce(out=node_visits[:], in_=visits[:], axis=AX.X, op=ALU.add)
+        nc.vector.tensor_scalar(out=visits1[:], in0=visits[:], scalar1=1.0, scalar2=None, op0=ALU.add)
+        nc.vector.reciprocal(out=inv_visits[:], in_=visits1[:])
+        nc.gpsimd.memset(one_half[:], 0.5)
+        nc.gpsimd.tensor_scalar(out=node_visits1[:], in0=node_visits[:], scalar1=1.0, scalar2=None, op0=ALU.add)
+        nc.gpsimd.tensor_tensor(out=root[:], in0=node_visits1[:], in1=one_half[:], op=ALU.pow)
+
+        x_codes = [keep.tile([P, HALF], U32, name="x_codes%d" % h, align_bytes=64) for h in range(HALVES)]
+        x_bytes = [keep.tile([P, HALF], U8, name="x_bytes%d" % h, align_bytes=64) for h in range(HALVES)]
+        lists = [offsets[:, h * (HALF // 16) : (h + 1) * (HALF // 16)] for h in range(HALVES)]
+        for h in range(HALVES):
+            nc.vector.tensor_copy(x_bytes[h][:], table_scales[:].indirect(lists[h]))
+
+        w_codes = []
+        w_bytes = []
+        for b in range(BLOCKS):
+            w_grouped = keep.tile([P, P, PACK], BF16, name="w_grouped%d" % b, align_bytes=64)
+            nc.scalar.copy(out=w_grouped[:], in_=w_raw[:, :, b * P : (b + 1) * P].rearrange("p j m -> p m j"))
+            codes = keep.tile([P, P], U32, name="w_codes%d" % b, align_bytes=64)
+            scales = keep.tile([P, P], U8, name="w_bytes%d" % b, align_bytes=64)
+            nc.vector.quantize_mx(out=codes[:].bitcast(FP8X4), scales=scales[:], in_=w_grouped[:].rearrange("p m j -> p (m j)"))
+            w_codes.append(codes)
+            w_bytes.append(scales)
+
+        chunks = [(h, b) for h in range(HALVES) for b in range(BLOCKS)]
+        for h in range(HALVES):
+            nc.vector.tensor_copy(x_codes[h][:], table_words[:].indirect(lists[h]))
+            for b in range(BLOCKS):
+                nc.tensor.matmul_mx(
+                    out=banks[BLOCKS * h + b][:],
+                    lhsT=w_codes[b][:].bitcast(FP8X4),
+                    lhsT_scale=w_bytes[b][:],
+                    rhs=x_codes[h][:].bitcast(FP8X4),
+                    rhs_scale=x_bytes[h][:],
+                    start=True,
+                    stop=True,
+                )
+
+        turned_banks = [(banks[4], banks[5]), (banks[0], banks[1])]
+        total_banks = [banks[6], banks[7]]
+        back_banks = [(banks[2], banks[3]), (banks[4], banks[5])]
+
+        def largest(h, b):
+            top = keep.tile([P, P], F32, name="top%d%d" % (h, b))
+            nc.vector.tensor_reduce(out=top[:], in_=banks[BLOCKS * h + b][:].rearrange("p (v d) -> p v d", d=D), axis=AX.X, op=ALU.max)
+            return top
+
+        def exponentials(h, b, top):
+            y = banks[BLOCKS * h + b]
+            shifted = keep.tile([P, D, P], F32, name="shifted%d%d" % (h, b))
+            nc.vector.tensor_tensor(out=shifted[:], in0=y[:].rearrange("p (v d) -> p d v", d=D), in1=top[:].unsqueeze(1).to_broadcast([P, D, P]), op=ALU.subtract)
+            ex = keep.tile([P, D, P], F32, name="ex%d%d" % (h, b))
+            nc.scalar.activation(out=ex[:], in_=shifted[:], func=ACT.Exp)
+            return ex
+
+        def turn_sum(h, b, ex):
+            other = BLOCKS - 1 - b
+            for d in range(D):
+                nc.tensor.matmul(out=total_banks[h][:, other * P : (other + 1) * P], lhsT=ex[:, d, :], rhs=ident[:], is_transpose=True, start=(d == 0), stop=(d == D - 1))
+
+        def turn_ex(h, b, ex):
+            for d in range(D):
+                col = (d % 2) * N + b * P
+                nc.tensor.transpose(turned_banks[h][d // 2][:, col : col + P], ex[:, d, :], ident[:])
+
+        factors = [keep.tile([P, 2, P], F32, name="factor%d" % h) for h in range(HALVES)]
+        bonus = [[keep.tile([P, N], F32, name="bonus%d%d" % (h, d)) for d in range(D)] for h in range(HALVES)]
+
+        def inversion_steps(h):
+            totals = total_banks[h][:, 0:N].rearrange("p (a n) -> p a n", a=2)
+            pair = keep.tile([P, 2, P // 2], F32, name="pair%d" % h)
+            quad = keep.tile([P, P // 2], F32, name="quad%d" % h)
+            inv_quad = keep.tile([P, P // 2], F32, name="inv_quad%d" % h)
+            inv_pair = keep.tile([P, 2, P // 2], F32, name="inv_pair%d" % h)
+            return [
+                lambda: nc.vector.tensor_reduce(out=pair[:].rearrange("p a n -> p (a n)"), in_=totals.rearrange("p a n -> p n a"), axis=AX.X, op=ALU.mult),
+                lambda: nc.vector.tensor_tensor(out=quad[:], in0=pair[:, 0, :], in1=pair[:, 1, :], op=ALU.mult),
+                lambda: nc.vector.reciprocal(out=inv_quad[:], in_=quad[:]),
+                lambda: nc.vector.tensor_tensor(out=inv_pair[:], in0=pair[:, ::-1, :], in1=inv_quad[:].unsqueeze(1).to_broadcast([P, 2, P // 2]), op=ALU.mult),
+                lambda: nc.vector.scalar_tensor_tensor(
+                    out=factors[h][:], in0=totals, scalar=root[:, h : h + 1],
+                    in1=inv_pair[:].rearrange("p a n -> p (a n)").unsqueeze(1).to_broadcast([P, 2, P]), op0=ALU.mult, op1=ALU.mult),
+            ]
+
+        def scale_and_turn_back(h, d):
+            col = (d % 2) * N
+            nc.vector.scalar_tensor_tensor(
+                out=bonus[h][d][:], in0=turned_banks[h][d // 2][:, col : col + N], scalar=inv_visits[:, h, d : d + 1],
+                in1=factors[h][:].rearrange("p a n -> p (a n)"), op0=ALU.mult, op1=ALU.mult)
+            for b in range(BLOCKS):
+                nc.tensor.transpose(back_banks[h][b][:, d * P : (d + 1) * P], bonus[h][d][:, b * P : (b + 1) * P], ident[:])
+
+        def finish(h, b):
+            result = keep.tile([P, P, D], F32, name="result%d%d" % (h, b))
+            turned = back_banks[h][b][:].rearrange("p (d v) -> p v d", d=D)
+            cols = slice(h * HALF, (h + 1) * HALF)
+            if h < 1:
+                scaled = keep.tile([P, P, D], F32, name="scaled%d%d" % (h, b))
+                nc.scalar.activation(out=scaled[:], in_=turned, func=ACT.Copy, scale=explore[:, b : b + 1])
+                nc.gpsimd.tensor_tensor(out=result[:].rearrange("p v d -> p (v d)"), in0=scaled[:].rearrange("p v d -> p (v d)"), in1=values[b][:, cols], op=ALU.add)
+            else:
+                nc.vector.scalar_tensor_tensor(
+                    out=result[:], in0=turned, scalar=explore[:, b : b + 1],
+                    in1=values[b][:, cols].rearrange("p (v d) -> p v d", d=D), op0=ALU.mult, op1=ALU.add)
+            nc.sync.dma_start(out=out[b * P : (b + 1) * P, cols], in_=result[:].rearrange("p v d -> p (v d)"))
+
+        for h in range(HALVES):
+            tops = [largest(h, b) for b in range(BLOCKS)]
+            exs = [exponentials(h, b, tops[b]) for b in range(BLOCKS)]
+            for b in range(BLOCKS):
+                turn_sum(h, b, exs[b])
+            for b in range(BLOCKS):
+                turn_ex(h, b, exs[b])
+        for step in inversion_steps(0):
+            step()
+        steps = inversion_steps(1)
+        for d in range(D):
+            scale_and_turn_back(0, d)
+            steps[d]()
+        steps[D]()
+        for b in range(BLOCKS):
+            finish(0, b)
+        for d in range(D):
+            scale_and_turn_back(1, d)
+        for b in range(BLOCKS):
+            finish(1, b)

@@ -38,19 +38,20 @@ def tile_picked_ypuct_puct_p_kernel(tc, x_words, x_scales, w1, cnt, qv, cpu, off
         visits = keep.tile([P, HALVES, D], F32, name="visits")
         nc.sync.dma_start(out=visits[:], in_=cnt[0, :].rearrange("(h p d) -> p h d", h=HALVES, d=D))
 
+        w_raw = keep.tile([P, PACK, N], F32, name="w_raw")
+        nc.sync.dma_start(out=w_raw[:], in_=w1.rearrange("(p j) m -> p j m", j=PACK))
         table_scales = keep.tile([P, T], U8, name="table_scales", align_bytes=64)
-        nc.vector.memset(table_scales[:].bitcast(I32), 0)
+        nc.gpsimd.memset(table_scales[:].bitcast(I32), 0)
         for q in range(4):
             nc.sync.dma_start(out=table_scales[32 * q : 32 * q + 4, :].bitcast(I32), in_=x_scales[0, 4 * q : 4 * q + 4, :].bitcast(I32))
 
-        w_raw = keep.tile([P, PACK, N], F32, name="w_raw")
-        nc.sync.dma_start(out=w_raw[:], in_=w1.rearrange("(p j) m -> p j m", j=PACK))
         table_words = keep.tile([P, T], U32, name="table_words", align_bytes=64)
         nc.sync.dma_start(out=table_words[:].bitcast(I32), in_=x_words[0].rearrange("p c r -> p (c r)").bitcast(I32))
 
         explore = keep.tile([P, BLOCKS], F32, name="explore")
         with nc.allow_non_contiguous_dma(reason="one value a partition"):
             nc.sync.dma_start(out=explore[:], in_=cpu.rearrange("(b p) o -> p (b o)", b=BLOCKS))
+
         values = [keep.tile([P, S], F32, name="values%d" % b) for b in range(BLOCKS)]
         for b in range(BLOCKS):
             nc.sync.dma_start(out=values[b][:], in_=qv[b * P : (b + 1) * P, :])
@@ -70,23 +71,24 @@ def tile_picked_ypuct_puct_p_kernel(tc, x_words, x_scales, w1, cnt, qv, cpu, off
         nc.gpsimd.memset(one_half[:], 0.5)
         nc.gpsimd.tensor_scalar(out=node_visits1[:], in0=node_visits[:], scalar1=1.0, scalar2=None, op0=ALU.add)
         nc.gpsimd.tensor_tensor(out=root[:], in0=node_visits1[:], in1=one_half[:], op=ALU.pow)
+        gain = keep.tile([P, HALVES, D], F32, name="gain")
+        nc.gpsimd.tensor_tensor(out=gain[:], in0=inv_visits[:], in1=root[:].unsqueeze(2).to_broadcast([P, HALVES, D]), op=ALU.mult)
 
-        x_codes = [keep.tile([P, HALF], U32, name="x_codes%d" % h, align_bytes=64) for h in range(HALVES)]
         x_bytes = [keep.tile([P, HALF], U8, name="x_bytes%d" % h, align_bytes=64) for h in range(HALVES)]
         lists = [offsets[:, h * (HALF // 16) : (h + 1) * (HALF // 16)] for h in range(HALVES)]
         for h in range(HALVES):
             nc.vector.tensor_copy(x_bytes[h][:], table_scales[:].indirect(lists[h]))
 
-        w_codes = []
-        w_bytes = []
+        w_grouped = keep.tile([P, N, PACK], BF16, name="w_grouped", tag="staging", align_bytes=64)
         for b in range(BLOCKS):
-            w_grouped = keep.tile([P, P, PACK], BF16, name="w_grouped%d" % b, align_bytes=64)
-            nc.scalar.copy(out=w_grouped[:], in_=w_raw[:, :, b * P : (b + 1) * P].rearrange("p j m -> p m j"))
-            codes = keep.tile([P, P], U32, name="w_codes%d" % b, align_bytes=64)
-            scales = keep.tile([P, P], U8, name="w_bytes%d" % b, align_bytes=64)
-            nc.vector.quantize_mx(out=codes[:].bitcast(FP8X4), scales=scales[:], in_=w_grouped[:].rearrange("p m j -> p (m j)"))
-            w_codes.append(codes)
-            w_bytes.append(scales)
+            nc.scalar.copy(out=w_grouped[:, b * P : (b + 1) * P, :], in_=w_raw[:, :, b * P : (b + 1) * P].rearrange("p j m -> p m j"))
+        w_codes = keep.tile([P, N], U32, name="w_codes", align_bytes=64)
+        w_bytes = keep.tile([P, N], U8, name="w_bytes", align_bytes=64)
+        nc.vector.quantize_mx(out=w_codes[:].bitcast(FP8X4), scales=w_bytes[:], in_=w_grouped[:].rearrange("p m j -> p (m j)"))
+        x_codes = [
+            keep.tile([P, HALF], U32, name="x_codes0", align_bytes=64),
+            keep.tile([P, HALF], U32, name="x_codes1", tag="staging", align_bytes=64),
+        ]
 
         chunks = [(h, b) for h in range(HALVES) for b in range(BLOCKS)]
         for h in range(HALVES):
@@ -94,99 +96,90 @@ def tile_picked_ypuct_puct_p_kernel(tc, x_words, x_scales, w1, cnt, qv, cpu, off
             for b in range(BLOCKS):
                 nc.tensor.matmul_mx(
                     out=banks[BLOCKS * h + b][:],
-                    lhsT=w_codes[b][:].bitcast(FP8X4),
-                    lhsT_scale=w_bytes[b][:],
+                    lhsT=w_codes[:, b * P : (b + 1) * P].bitcast(FP8X4),
+                    lhsT_scale=w_bytes[:, b * P : (b + 1) * P],
                     rhs=x_codes[h][:].bitcast(FP8X4),
                     rhs_scale=x_bytes[h][:],
                     start=True,
                     stop=True,
                 )
 
-        turned_banks = [(banks[4], banks[5]), (banks[0], banks[1])]
+        turned_banks = [[banks[4], banks[5]], [banks[0], banks[1]]]
         total_banks = [banks[6], banks[7]]
-        back_banks = [(banks[2], banks[3]), (banks[4], banks[5])]
+        back_banks = [[banks[2], banks[3]], [banks[4], banks[5]]]
+        tops = [keep.tile([P, P], F32, name="top%d" % b) for b in range(BLOCKS)]
+        factors = [keep.tile([P, BLOCKS, P], F32, name="factor%d" % h) for h in range(HALVES)]
 
         def largest(h, b):
-            top = keep.tile([P, P], F32, name="top%d%d" % (h, b))
-            nc.vector.tensor_reduce(out=top[:], in_=banks[BLOCKS * h + b][:].rearrange("p (v d) -> p v d", d=D), axis=AX.X, op=ALU.max)
-            return top
+            nc.vector.tensor_reduce(out=tops[b][:], in_=banks[BLOCKS * h + b][:].rearrange("p (v d) -> p v d", d=D), axis=AX.X, op=ALU.max)
 
-        def exponentials(h, b, top):
+        def exponentials(h, b):
             y = banks[BLOCKS * h + b]
             shifted = keep.tile([P, D, P], F32, name="shifted%d%d" % (h, b))
-            nc.vector.tensor_tensor(out=shifted[:], in0=y[:].rearrange("p (v d) -> p d v", d=D), in1=top[:].unsqueeze(1).to_broadcast([P, D, P]), op=ALU.subtract)
+            nc.vector.tensor_tensor(out=shifted[:], in0=y[:].rearrange("p (v d) -> p d v", d=D), in1=tops[b][:].unsqueeze(1).to_broadcast([P, D, P]), op=ALU.subtract)
             ex = keep.tile([P, D, P], F32, name="ex%d%d" % (h, b))
             nc.scalar.activation(out=ex[:], in_=shifted[:], func=ACT.Exp)
             return ex
 
         def turn_sum(h, b, ex):
-            other = BLOCKS - 1 - b
+            place = BLOCKS - 1 - b if h == 0 else b
             for d in range(D):
-                nc.tensor.matmul(out=total_banks[h][:, other * P : (other + 1) * P], lhsT=ex[:, d, :], rhs=ident[:], is_transpose=True, start=(d == 0), stop=(d == D - 1))
+                nc.tensor.matmul(out=total_banks[h][:, place * P : (place + 1) * P], lhsT=ex[:, d, :], rhs=ident[:], is_transpose=True, start=(d == 0), stop=(d == D - 1))
 
         def turn_ex(h, b, ex):
             for d in range(D):
-                col = (d % 2) * N + b * P
-                nc.tensor.transpose(turned_banks[h][d // 2][:, col : col + P], ex[:, d, :], ident[:])
+                nc.tensor.transpose(turned_banks[h][b][:, d * P : (d + 1) * P], ex[:, d, :], ident[:])
 
-        factors = [keep.tile([P, 2, P], F32, name="factor%d" % h) for h in range(HALVES)]
-        bonus = [[keep.tile([P, N], F32, name="bonus%d%d" % (h, d)) for d in range(D)] for h in range(HALVES)]
+        def invert_on_vector(h):
+            totals = total_banks[h][:, 0:N].rearrange("p (a n) -> p a n", a=BLOCKS)
+            parts = [slice(i * (P // 2), (i + 1) * (P // 2)) for i in range(2)]
+            pair = keep.tile([P, P], F32, name="pair")
+            inv_pair = keep.tile([P, P], F32, name="inv_pair")
+            for cols in parts:
+                nc.vector.tensor_reduce(out=pair[:, cols], in_=totals[:, :, cols].rearrange("p a n -> p n a"), axis=AX.X, op=ALU.mult)
+            for cols in parts:
+                nc.vector.reciprocal(out=inv_pair[:, cols], in_=pair[:, cols])
+            for cols in parts:
+                nc.vector.tensor_tensor(out=factors[h][:, :, cols], in0=totals[:, :, cols], in1=inv_pair[:, cols].unsqueeze(1).to_broadcast([P, BLOCKS, P // 2]), op=ALU.mult)
 
-        def inversion_steps(h):
-            totals = total_banks[h][:, 0:N].rearrange("p (a n) -> p a n", a=2)
-            pair = keep.tile([P, 2, P // 2], F32, name="pair%d" % h)
-            quad = keep.tile([P, P // 2], F32, name="quad%d" % h)
-            inv_quad = keep.tile([P, P // 2], F32, name="inv_quad%d" % h)
-            inv_pair = keep.tile([P, 2, P // 2], F32, name="inv_pair%d" % h)
-            return [
-                lambda: nc.vector.tensor_reduce(out=pair[:].rearrange("p a n -> p (a n)"), in_=totals.rearrange("p a n -> p n a"), axis=AX.X, op=ALU.mult),
-                lambda: nc.vector.tensor_tensor(out=quad[:], in0=pair[:, 0, :], in1=pair[:, 1, :], op=ALU.mult),
-                lambda: nc.vector.reciprocal(out=inv_quad[:], in_=quad[:]),
-                lambda: nc.vector.tensor_tensor(out=inv_pair[:], in0=pair[:, ::-1, :], in1=inv_quad[:].unsqueeze(1).to_broadcast([P, 2, P // 2]), op=ALU.mult),
-                lambda: nc.vector.scalar_tensor_tensor(
-                    out=factors[h][:], in0=totals, scalar=root[:, h : h + 1],
-                    in1=inv_pair[:].rearrange("p a n -> p (a n)").unsqueeze(1).to_broadcast([P, 2, P]), op0=ALU.mult, op1=ALU.mult),
-            ]
-
-        def scale_and_turn_back(h, d):
-            col = (d % 2) * N
-            nc.vector.scalar_tensor_tensor(
-                out=bonus[h][d][:], in0=turned_banks[h][d // 2][:, col : col + N], scalar=inv_visits[:, h, d : d + 1],
-                in1=factors[h][:].rearrange("p a n -> p (a n)"), op0=ALU.mult, op1=ALU.mult)
+        def invert_on_scalar(h):
+            inv_root = keep.tile([P, BLOCKS, P], F32, name="inv_root")
             for b in range(BLOCKS):
-                nc.tensor.transpose(back_banks[h][b][:, d * P : (d + 1) * P], bonus[h][d][:, b * P : (b + 1) * P], ident[:])
+                nc.scalar.activation(out=inv_root[:, b, :], in_=total_banks[h][:, b * P : (b + 1) * P], func=ACT.Abs_reciprocal_sqrt)
+            for b in range(BLOCKS):
+                nc.scalar.activation(out=factors[h][:, b, :], in_=inv_root[:, b, :], func=ACT.Square)
 
-        def finish(h, b):
-            result = keep.tile([P, P, D], F32, name="result%d%d" % (h, b))
-            turned = back_banks[h][b][:].rearrange("p (d v) -> p v d", d=D)
-            cols = slice(h * HALF, (h + 1) * HALF)
-            if h < 1:
-                scaled = keep.tile([P, P, D], F32, name="scaled%d%d" % (h, b))
-                nc.scalar.activation(out=scaled[:], in_=turned, func=ACT.Copy, scale=explore[:, b : b + 1])
-                nc.gpsimd.tensor_tensor(out=result[:].rearrange("p v d -> p (v d)"), in0=scaled[:].rearrange("p v d -> p (v d)"), in1=values[b][:, cols], op=ALU.add)
-            else:
+        def scale_and_turn_back(h, b):
+            for d in range(D):
+                bonus = keep.tile([P, P], F32, name="bonus%d%d%d" % (h, b, d))
                 nc.vector.scalar_tensor_tensor(
-                    out=result[:], in0=turned, scalar=explore[:, b : b + 1],
+                    out=bonus[:], in0=turned_banks[h][b][:, d * P : (d + 1) * P], scalar=gain[:, h, d : d + 1],
+                    in1=factors[h][:, b, :], op0=ALU.mult, op1=ALU.mult)
+                nc.tensor.transpose(back_banks[h][b][:, d * P : (d + 1) * P], bonus[:], ident[:])
+
+        def finish(h, b, pieces=1):
+            turned = back_banks[h][b][:].rearrange("p (d v) -> p v d", d=D)
+            nodes = P // pieces
+            for i in range(pieces):
+                result = keep.tile([P, nodes, D], F32, name="result%d%d%d" % (h, b, i))
+                cols = slice(h * HALF + i * nodes * D, h * HALF + (i + 1) * nodes * D)
+                nc.vector.scalar_tensor_tensor(
+                    out=result[:], in0=turned[:, i * nodes : (i + 1) * nodes, :], scalar=explore[:, b : b + 1],
                     in1=values[b][:, cols].rearrange("p (v d) -> p v d", d=D), op0=ALU.mult, op1=ALU.add)
-            nc.sync.dma_start(out=out[b * P : (b + 1) * P, cols], in_=result[:].rearrange("p v d -> p (v d)"))
+                nc.sync.dma_start(out=out[b * P : (b + 1) * P, cols], in_=result[:].rearrange("p v d -> p (v d)"))
 
         for h in range(HALVES):
-            tops = [largest(h, b) for b in range(BLOCKS)]
-            exs = [exponentials(h, b, tops[b]) for b in range(BLOCKS)]
+            for b in range(BLOCKS):
+                largest(h, b)
+            exs = [exponentials(h, b) for b in range(BLOCKS)]
             for b in range(BLOCKS):
                 turn_sum(h, b, exs[b])
             for b in range(BLOCKS):
                 turn_ex(h, b, exs[b])
-        for step in inversion_steps(0):
-            step()
-        steps = inversion_steps(1)
-        for d in range(D):
-            scale_and_turn_back(0, d)
-            steps[d]()
-        steps[D]()
-        for b in range(BLOCKS):
-            finish(0, b)
-        for d in range(D):
-            scale_and_turn_back(1, d)
-        for b in range(BLOCKS):
-            finish(1, b)
+        invert_on_vector(0)
+        invert_on_scalar(1)
+        scale_and_turn_back(*chunks[0])
+        for i in range(1, len(chunks)):
+            scale_and_turn_back(*chunks[i])
+            finish(*chunks[i - 1])
+        finish(*chunks[-1], pieces=2)

@@ -32,18 +32,18 @@ def tile_picked_ypuct_puct_p_kernel(tc, x_words, x_scales, w1, cnt, qv, cpu, off
         psum = ctx.enter_context(tc.psum_pool(name="psum", bufs=1))
         banks = [psum.tile([P, HALF], F32, name="bank%d" % i) for i in range(8)]
 
-        offsets = keep.tile([P, S // 16], U16, name="offsets")
-        nc.sync.dma_start(offsets[:], offs)
-
         visits = keep.tile([P, HALVES, D], F32, name="visits")
         nc.sync.dma_start(out=visits[:], in_=cnt[0, :].rearrange("(h p d) -> p h d", h=HALVES, d=D))
 
+        offsets = keep.tile([P, S // 16], U16, name="offsets")
+        nc.sync.dma_start(offsets[:], offs)
+
         w_raw = keep.tile([P, PACK, N], F32, name="w_raw")
-        nc.sync.dma_start(out=w_raw[:], in_=w1.rearrange("(p j) m -> p j m", j=PACK))
+        nc.scalar.dma_start(out=w_raw[:], in_=w1.rearrange("(p j) m -> p j m", j=PACK))
         table_scales = keep.tile([P, T], U8, name="table_scales", align_bytes=64)
-        nc.gpsimd.memset(table_scales[:].bitcast(I32), 0)
-        for q in range(4):
-            nc.sync.dma_start(out=table_scales[32 * q : 32 * q + 4, :].bitcast(I32), in_=x_scales[0, 4 * q : 4 * q + 4, :].bitcast(I32))
+        nc.vector.memset(table_scales[:].bitcast(I32), 0)
+        for r in range(4):
+            nc.sync.dma_start(out=table_scales[r:P:32, :].bitcast(I32), in_=x_scales[0, r:16:4, :].bitcast(I32))
 
         table_words = keep.tile([P, T], U32, name="table_words", align_bytes=64)
         nc.sync.dma_start(out=table_words[:].bitcast(I32), in_=x_words[0].rearrange("p c r -> p (c r)").bitcast(I32))
@@ -67,12 +67,13 @@ def tile_picked_ypuct_puct_p_kernel(tc, x_words, x_scales, w1, cnt, qv, cpu, off
         root = keep.tile([P, HALVES], F32, name="root")
         nc.vector.tensor_reduce(out=node_visits[:], in_=visits[:], axis=AX.X, op=ALU.add)
         nc.vector.tensor_scalar(out=visits1[:], in0=visits[:], scalar1=1.0, scalar2=None, op0=ALU.add)
-        nc.vector.reciprocal(out=inv_visits[:], in_=visits1[:])
         nc.gpsimd.memset(one_half[:], 0.5)
-        nc.gpsimd.tensor_scalar(out=node_visits1[:], in0=node_visits[:], scalar1=1.0, scalar2=None, op0=ALU.add)
+        nc.vector.tensor_scalar(out=node_visits1[:], in0=node_visits[:], scalar1=1.0, scalar2=None, op0=ALU.add)
+        nc.vector.reciprocal(out=inv_visits[:], in_=visits1[:])
         nc.gpsimd.tensor_tensor(out=root[:], in0=node_visits1[:], in1=one_half[:], op=ALU.pow)
         gain = keep.tile([P, HALVES, D], F32, name="gain")
-        nc.gpsimd.tensor_tensor(out=gain[:], in0=inv_visits[:], in1=root[:].unsqueeze(2).to_broadcast([P, HALVES, D]), op=ALU.mult)
+        for h in range(HALVES):
+            nc.scalar.activation(out=gain[:, h, :], in_=inv_visits[:, h, :], func=ACT.Copy, scale=root[:, h : h + 1])
 
         x_bytes = [keep.tile([P, HALF], U8, name="x_bytes%d" % h, align_bytes=64) for h in range(HALVES)]
         lists = [offsets[:, h * (HALF // 16) : (h + 1) * (HALF // 16)] for h in range(HALVES)]
@@ -104,9 +105,9 @@ def tile_picked_ypuct_puct_p_kernel(tc, x_words, x_scales, w1, cnt, qv, cpu, off
                     stop=True,
                 )
 
-        turned_banks = [[banks[4], banks[5]], [banks[0], banks[1]]]
+        turned_banks = [[banks[2], banks[5]], [banks[0], banks[2]]]
         total_banks = [banks[6], banks[7]]
-        back_banks = [[banks[2], banks[3]], [banks[4], banks[5]]]
+        back_banks = [[banks[4], banks[3]], [banks[1], banks[5]]]
         tops = [keep.tile([P, P], F32, name="top%d" % b) for b in range(BLOCKS)]
         factors = [keep.tile([P, BLOCKS, P], F32, name="factor%d" % h) for h in range(HALVES)]
 
@@ -168,17 +169,20 @@ def tile_picked_ypuct_puct_p_kernel(tc, x_words, x_scales, w1, cnt, qv, cpu, off
                     in1=values[b][:, cols].rearrange("p (v d) -> p v d", d=D), op0=ALU.mult, op1=ALU.add)
                 nc.sync.dma_start(out=out[b * P : (b + 1) * P, cols], in_=result[:].rearrange("p v d -> p (v d)"))
 
+        exs = {}
         for h in range(HALVES):
             for b in range(BLOCKS):
                 largest(h, b)
-            exs = [exponentials(h, b) for b in range(BLOCKS)]
             for b in range(BLOCKS):
-                turn_sum(h, b, exs[b])
+                exs[h, b] = exponentials(h, b)
             for b in range(BLOCKS):
-                turn_ex(h, b, exs[b])
+                turn_sum(h, b, exs[h, b])
+        for h, b in chunks[:-1]:
+            turn_ex(h, b, exs[h, b])
         invert_on_vector(0)
         invert_on_scalar(1)
         scale_and_turn_back(*chunks[0])
+        turn_ex(*chunks[-1], exs[chunks[-1]])
         for i in range(1, len(chunks)):
             scale_and_turn_back(*chunks[i])
             finish(*chunks[i - 1])

from contextlib import ExitStack

import concourse.mybir as mybir
from concourse.masks import make_identity

K, T, S, D, N = 512, 2048, 1024, 4, 256
FLOPS = 2 * K * N * S
BYTES = K * T + (K // 32) * T + 4 * K * N + 4 * S + 4 * N * S + 4 * N + 128 * (S // 16) * 2 + 4 * N * S

F32 = mybir.dt.float32
BF16 = mybir.dt.bfloat16
I32 = mybir.dt.int32
U32 = mybir.dt.uint32
U16 = mybir.dt.uint16
U8 = mybir.dt.uint8
FP8X4 = mybir.dt.float8_e4m3fn_x4
ALU = mybir.AluOpType
ACT = mybir.ActivationFunctionType
AX = mybir.AxisListType

P = 128
PACK = 4
HALF = 512
HALVES = S // HALF
BLOCKS = N // P


def tile_picked_ypuct_puct_p_kernel(tc, x_words, x_scales, w1, cnt, qv, cpu, offs, out):
    nc = tc.nc
    with ExitStack() as ctx:
        keep = ctx.enter_context(tc.tile_pool(name="keep", bufs=1))
        psum = ctx.enter_context(tc.psum_pool(name="psum", bufs=1))
        banks = [psum.tile([P, HALF], F32, name="bank%d" % i) for i in range(8)]

        visits = keep.tile([P, HALVES, D], F32, name="visits")
        nc.sync.dma_start(out=visits[:], in_=cnt[0, :].rearrange("(h p d) -> p h d", h=HALVES, d=D))

        offsets = keep.tile([P, S // 16], U16, name="offsets")
        nc.sync.dma_start(offsets[:], offs)

        w_raw = keep.tile([P, PACK, N], F32, name="w_raw")
        nc.scalar.dma_start(out=w_raw[:], in_=w1.rearrange("(p j) m -> p j m", j=PACK))
        table_scales = keep.tile([P, T], U8, name="table_scales", align_bytes=64)
        nc.vector.memset(table_scales[:].bitcast(I32), 0)
        for r in range(4):
            nc.sync.dma_start(out=table_scales[r:P:32, :].bitcast(I32), in_=x_scales[0, r:16:4, :].bitcast(I32))

        table_words = keep.tile([P, T], U32, name="table_words", align_bytes=64)
        nc.sync.dma_start(out=table_words[:].bitcast(I32), in_=x_words[0].rearrange("p c r -> p (c r)").bitcast(I32))

        explore = keep.tile([P, BLOCKS], F32, name="explore")
        with nc.allow_non_contiguous_dma(reason="one value a partition"):
            nc.sync.dma_start(out=explore[:], in_=cpu.rearrange("(b p) o -> p (b o)", b=BLOCKS))

        values = [keep.tile([P, S], F32, name="values%d" % b) for b in range(BLOCKS)]
        for b in range(BLOCKS):
            nc.sync.dma_start(out=values[b][:], in_=qv[b * P : (b + 1) * P, :])

        ident = keep.tile([P, P], F32, name="ident")
        make_identity(nc, ident[:])

        visits1 = keep.tile([P, HALVES, D], F32, name="visits1")
        inv_visits = keep.tile([P, HALVES, D], F32, name="inv_visits")
        node_visits = keep.tile([P, HALVES], F32, name="node_visits")
        node_visits1 = keep.tile([P, HALVES], F32, name="node_visits1")
        one_half = keep.tile([P, HALVES], F32, name="one_half")
        root = keep.tile([P, HALVES], F32, name="root")
        nc.vector.tensor_reduce(out=node_visits[:], in_=visits[:], axis=AX.X, op=ALU.add)
        nc.vector.tensor_scalar(out=visits1[:], in0=visits[:], scalar1=1.0, scalar2=None, op0=ALU.add)
        nc.gpsimd.memset(one_half[:], 0.5)
        nc.vector.tensor_scalar(out=node_visits1[:], in0=node_visits[:], scalar1=1.0, scalar2=None, op0=ALU.add)
        nc.vector.reciprocal(out=inv_visits[:], in_=visits1[:])
        nc.gpsimd.tensor_tensor(out=root[:], in0=node_visits1[:], in1=one_half[:], op=ALU.pow)
        gain = keep.tile([P, HALVES, D], F32, name="gain")
        for h in range(HALVES):
            nc.scalar.activation(out=gain[:, h, :], in_=inv_visits[:, h, :], func=ACT.Copy, scale=root[:, h : h + 1])

        x_bytes = [keep.tile([P, HALF], U8, name="x_bytes%d" % h, align_bytes=64) for h in range(HALVES)]
        lists = [offsets[:, h * (HALF // 16) : (h + 1) * (HALF // 16)] for h in range(HALVES)]
        for h in range(HALVES):
            nc.vector.tensor_copy(x_bytes[h][:], table_scales[:].indirect(lists[h]))

        w_grouped = keep.tile([P, N, PACK], BF16, name="w_grouped", tag="staging", align_bytes=64)
        for b in range(BLOCKS):
            nc.scalar.copy(out=w_grouped[:, b * P : (b + 1) * P, :], in_=w_raw[:, :, b * P : (b + 1) * P].rearrange("p j m -> p m j"))
        w_codes = keep.tile([P, N], U32, name="w_codes", align_bytes=64)
        w_bytes = keep.tile([P, N], U8, name="w_bytes", align_bytes=64)
        nc.vector.quantize_mx(out=w_codes[:].bitcast(FP8X4), scales=w_bytes[:], in_=w_grouped[:].rearrange("p m j -> p (m j)"))
        x_codes = [
            keep.tile([P, HALF], U32, name="x_codes0", align_bytes=64),
            keep.tile([P, HALF], U32, name="x_codes1", tag="staging", align_bytes=64),
        ]

        chunks = [(h, b) for h in range(HALVES) for b in range(BLOCKS)]
        for h in range(HALVES):
            nc.vector.tensor_copy(x_codes[h][:], table_words[:].indirect(lists[h]))
            for b in range(BLOCKS):
                nc.tensor.matmul_mx(
                    out=banks[BLOCKS * h + b][:],
                    lhsT=w_codes[:, b * P : (b + 1) * P].bitcast(FP8X4),
                    lhsT_scale=w_bytes[:, b * P : (b + 1) * P],
                    rhs=x_codes[h][:].bitcast(FP8X4),
                    rhs_scale=x_bytes[h][:],
                    start=True,
                    stop=True,
                )

        turned_banks = [[banks[2], banks[5]], [banks[0], banks[2]]]
        total_banks = [banks[6], banks[7]]
        back_banks = [[banks[4], banks[3]], [banks[1], banks[5]]]
        tops = [keep.tile([P, P], F32, name="top%d" % b) for b in range(BLOCKS)]
        factors = [keep.tile([P, BLOCKS, P], F32, name="factor%d" % h) for h in range(HALVES)]

        def largest(h, b):
            nc.vector.tensor_reduce(out=tops[b][:], in_=banks[BLOCKS * h + b][:].rearrange("p (v d) -> p v d", d=D), axis=AX.X, op=ALU.max)

        def exponentials(h, b):
            y = banks[BLOCKS * h + b]
            shifted = keep.tile([P, D, P], F32, name="shifted%d%d" % (h, b))
            nc.vector.tensor_tensor(out=shifted[:], in0=y[:].rearrange("p (v d) -> p d v", d=D), in1=tops[b][:].unsqueeze(1).to_broadcast([P, D, P]), op=ALU.subtract)
            ex = keep.tile([P, D, P], F32, name="ex%d%d" % (h, b))
            nc.scalar.activation(out=ex[:], in_=shifted[:], func=ACT.Exp)
            return ex

        def turn_sum(h, b, ex):
            place = BLOCKS - 1 - b if h == 0 else b
            for d in range(D):
                nc.tensor.matmul(out=total_banks[h][:, place * P : (place + 1) * P], lhsT=ex[:, d, :], rhs=ident[:], is_transpose=True, start=(d == 0), stop=(d == D - 1))

        def turn_ex(h, b, ex):
            for d in range(D):
                nc.tensor.transpose(turned_banks[h][b][:, d * P : (d + 1) * P], ex[:, d, :], ident[:])

        def invert_on_vector(h):
            totals = total_banks[h][:, 0:N].rearrange("p (a n) -> p a n", a=BLOCKS)
            parts = [slice(i * (P // 2), (i + 1) * (P // 2)) for i in range(2)]
            pair = keep.tile([P, P], F32, name="pair")
            inv_pair = keep.tile([P, P], F32, name="inv_pair")
            for cols in parts:
                nc.vector.tensor_reduce(out=pair[:, cols], in_=totals[:, :, cols].rearrange("p a n -> p n a"), axis=AX.X, op=ALU.mult)
            for cols in parts:
                nc.vector.reciprocal(out=inv_pair[:, cols], in_=pair[:, cols])
            for cols in parts:
                nc.vector.tensor_tensor(out=factors[h][:, :, cols], in0=totals[:, :, cols], in1=inv_pair[:, cols].unsqueeze(1).to_broadcast([P, BLOCKS, P // 2]), op=ALU.mult)

        def invert_on_scalar(h):
            inv_root = keep.tile([P, BLOCKS, P], F32, name="inv_root")
            for b in range(BLOCKS):
                nc.scalar.activation(out=inv_root[:, b, :], in_=total_banks[h][:, b * P : (b + 1) * P], func=ACT.Abs_reciprocal_sqrt)
            for b in range(BLOCKS):
                nc.scalar.activation(out=factors[h][:, b, :], in_=inv_root[:, b, :], func=ACT.Square)

        def scale_and_turn_back(h, b):
            for d in range(D):
                bonus = keep.tile([P, P], F32, name="bonus%d%d%d" % (h, b, d))
                nc.vector.scalar_tensor_tensor(
                    out=bonus[:], in0=turned_banks[h][b][:, d * P : (d + 1) * P], scalar=gain[:, h, d : d + 1],
                    in1=factors[h][:, b, :], op0=ALU.mult, op1=ALU.mult)
                nc.tensor.transpose(back_banks[h][b][:, d * P : (d + 1) * P], bonus[:], ident[:])

        def finish(h, b, pieces=1):
            turned = back_banks[h][b][:].rearrange("p (d v) -> p v d", d=D)
            nodes = P // pieces
            for i in range(pieces):
                result = keep.tile([P, nodes, D], F32, name="result%d%d%d" % (h, b, i))
                cols = slice(h * HALF + i * nodes * D, h * HALF + (i + 1) * nodes * D)
                nc.vector.scalar_tensor_tensor(
                    out=result[:], in0=turned[:, i * nodes : (i + 1) * nodes, :], scalar=explore[:, b : b + 1],
                    in1=values[b][:, cols].rearrange("p (v d) -> p v d", d=D), op0=ALU.mult, op1=ALU.add)
                nc.sync.dma_start(out=out[b * P : (b + 1) * P, cols], in_=result[:].rearrange("p v d -> p (v d)"))

        exs = {}
        for h in range(HALVES):
            for b in range(BLOCKS):
                largest(h, b)
            for b in range(BLOCKS):
                exs[h, b] = exponentials(h, b)
            for b in range(BLOCKS):
                turn_sum(h, b, exs[h, b])
        for h, b in chunks[:-1]:
            turn_ex(h, b, exs[h, b])
        invert_on_vector(0)
        invert_on_scalar(1)
        scale_and_turn_back(*chunks[0])
        turn_ex(*chunks[-1], exs[chunks[-1]])
        for i in range(1, len(chunks)):
            scale_and_turn_back(*chunks[i])
            finish(*chunks[i - 1])
        finish(*chunks[-1], pieces=2)
